import numpy as np
import ml_dtypes


def mxq(x, axis, fmt="e4m3"):
    dtype, down = {"e4m3": (ml_dtypes.float8_e4m3fn, 7), "e5m2": (ml_dtypes.float8_e5m2, 14)}[fmt]
    v = np.moveaxis(np.asarray(x, np.float32).astype(ml_dtypes.bfloat16).astype(np.float64), axis, -1)
    blocks = v.reshape(v.shape[:-1] + (-1, 32))
    amax = np.abs(blocks).max(-1, keepdims=True)
    byte = np.maximum(np.where(amax > 0, np.frexp(amax)[1] - 1 + 127, 0) - down, 1)
    scale = np.exp2(byte - 127.0)
    codes = (blocks / scale).astype(np.float32).astype(dtype).astype(np.float64)
    return np.moveaxis((codes * scale).reshape(v.shape), -1, axis)


WIDE = False


def mx_kscale(k):
    if not WIDE:
        return np.ones(k)
    levels = np.array([10, -10, 5, -5, 0])
    if k % 512:
        return np.exp2(np.random.permutation(np.resize(levels, k // 32))).repeat(32)
    a = np.empty((k // 512, 16))
    for p in range(k // 512):
        a[p, :8] = np.random.permutation(np.resize(levels, 8))
        for g in range(8):
            far = levels[np.abs(levels - a[p, g]) >= 10]
            a[p, g + 8] = far[np.random.randint(len(far))]
    return np.exp2(a.ravel()).repeat(32)


BF16 = ml_dtypes.bfloat16


def bf(x):
    return np.asarray(x, np.float32).astype(BF16)


def f64(x):
    return np.asarray(x).astype(np.float64)

def planes(Y):
    n, m = Y.shape
    b = f64(bf(Y)).reshape(n // 32, 32, m)
    amax = np.abs(b).max(1)
    byte = np.clip(np.where(amax > 0, np.frexp(amax)[1] - 1 + 127 - 7, 1), 1, 254)
    codes = (b * np.exp2(127.0 - byte)[:, None, :]).reshape(n, m).astype(np.float32).astype(ml_dtypes.float8_e4m3fn).view(np.uint8)
    words = codes.reshape(n // 512, 128, 4, m).transpose(0, 1, 3, 2)
    return np.ascontiguousarray(words), np.ascontiguousarray(byte.astype(np.uint8).reshape(n // 512, 16, m))


N, M, D, E = 1024, 2048, 512, 1024

EPS = 1e-6
U_SIZE = 0.005


def setup_inputs():
    s, t = mx_kscale(N), mx_kscale(D)
    ds = np.random.standard_normal((N, M)) * (U_SIZE * np.sqrt(D / N))
    q = 0.5 + np.random.standard_normal((N, D))
    u = (0.5 + np.random.standard_normal((M, D))) * U_SIZE
    gamma = 1.0 + 0.1 * np.random.standard_normal(D)
    l = 1.0 + 0.1 * np.random.standard_normal(D)
    wk = np.random.standard_normal((E, D)) / np.sqrt(D)
    return {"ds": bf(ds * s[:, None]), "q": bf(q / s[:, None]), "u": bf(u), "gamma": bf(gamma),
            "l": bf(l * t), "wk": bf(wk / t[None, :])}


def rms_norm_backward(u, gamma, dk):
    rho = np.sqrt(np.mean(u * u, axis=-1, keepdims=True) + EPS)
    uh = u / rho
    e = dk * gamma[None, :]
    return (e - uh * np.mean(e * uh, axis=-1, keepdims=True)) / rho


def core(ds, q, u, gamma, l, wk):
    dk = (mxq(f64(ds).T, 1, "e4m3") @ mxq(f64(q), 0, "e4m3")) / np.sqrt(D)
    du = rms_norm_backward(f64(u), f64(gamma), dk)
    dz = du * f64(l)[None, :]
    return mxq(dz, 1, "e4m3") @ mxq(f64(wk), 1, "e4m3").T


def reference(ds, q, u, gamma, l, wk):
    R_out = core(ds, q, u, gamma, l, wk)
    words, scales = planes(R_out.T)
    return R_out, words, scales

@@ -1,0 +1,332 @@
+from contextlib import ExitStack
+
+import concourse.mybir as mybir
+from concourse.masks import make_identity
+
+N, M, D, E = 1024, 2048, 512, 1024
+FLOPS = 2 * N * M * D + 2 * M * D * E
+
+F32 = mybir.dt.float32
+BF16 = mybir.dt.bfloat16
+U32 = mybir.dt.uint32
+I32 = mybir.dt.int32
+U8 = mybir.dt.uint8
+X4 = mybir.dt.float8_e4m3fn_x4
+ALU = mybir.AluOpType
+ACT = mybir.ActivationFunctionType
+
+P = 128
+EPS = 1e-6
+TILES = M // P
+UNIT = 256
+CHUNKS = [(0, 256), (256, 256), (512, 512), (1024, 512), (1536, 512)]
+
+
+def tile_ia3scaledqknormkeybackwardtoinput_x1_kernel(tc, ds, q, u, gamma, l, wk, out_0, out_1, out_2):
+    nc = tc.nc
+    with ExitStack() as ctx:
+        keep = ctx.enter_context(tc.tile_pool(name="keep", bufs=1))
+        work = ctx.enter_context(tc.tile_pool(name="work", bufs=3))
+        ps_dk = ctx.enter_context(tc.psum_pool(name="ps_dk", bufs=2))
+        ps_tr = ctx.enter_context(tc.psum_pool(name="ps_tr", bufs=2))
+        ps_out = ctx.enter_context(tc.psum_pool(name="ps_out", bufs=4))
+        ctx.enter_context(tc.manual_schedule())
+
+        q_raw = [keep.tile([P, 4, D], BF16, name="q_raw%d" % g) for g in range(2)]
+        ds_raw = [keep.tile([P, 2, 4, w], BF16, name="ds_raw%d" % c) for c, (a, w) in enumerate(CHUNKS)]
+        u_raw = [keep.tile([P, 2, D], BF16, name="u_raw%d" % c) for c in range(TILES // 2)]
+        wk_raw = keep.tile([P, 2, 4, D], BF16, name="wk_raw")
+        g_row = keep.tile([P, D], BF16, name="g_row")
+        ones = keep.tile([P, P], BF16, name="ones")
+        l_col = keep.tile([P, 4], BF16, name="l_col")
+        ident = keep.tile([P, P], F32, name="ident")
+        expo = keep.tile([P, 2], F32, name="expo")
+
+        def load_ds(c):
+            a, w = CHUNKS[c]
+            for g in range(2):
+                nc.sync.dma_start(
+                    out=ds_raw[c][:, g, :, :],
+                    in_=ds[512 * g : 512 * (g + 1), a : a + w].rearrange("(p j) m -> p j m", j=4),
+                )
+
+        def load_u(c):
+            nc.sync.dma_start(
+                out=u_raw[c][:], in_=u[256 * c : 256 * (c + 1), :].rearrange("(i p) d -> p i d", i=2)
+            )
+
+        nc.gpsimd.memset(g_row[:], 0.0)
+        nc.gpsimd.memset(ones[:], 1.0)
+        nc.gpsimd.memset(expo[:], -0.5)
+        make_identity(nc, ident[:])
+        nc.scalar.dma_start(out=l_col[:], in_=l.rearrange("(p t) -> p t", t=4))
+        nc.scalar.dma_start(out=g_row[0:1, :], in_=gamma.rearrange("(o d) -> o d", o=1))
+
+        for g in range(2):
+            nc.sync.dma_start(
+                out=q_raw[g][:], in_=q[512 * g : 512 * (g + 1), :].rearrange("(p j) d -> p j d", j=4)
+            )
+        load_ds(0)
+        load_u(0)
+        nc.sync.dma_start(out=wk_raw[:], in_=wk.rearrange("(g p t) d -> p g t d", g=2, t=4))
+        load_ds(1)
+        load_u(1)
+        load_ds(2)
+        load_u(2)
+        load_u(3)
+        load_ds(3)
+        load_u(4)
+        load_u(5)
+        load_ds(4)
+        load_u(6)
+        load_u(7)
+
+        def spread(x):
+            return x.rearrange("p (c i) t -> p c t i", i=4)
+
+        def gather(x):
+            return x.rearrange("p t (c i) -> p c t i", i=4)
+
+        qg = [keep.tile([P, D, 4], BF16, name="qg%d" % g, align_bytes=64) for g in range(2)]
+        qc = keep.tile([P, 2, D], U32, name="qc", align_bytes=64)
+        qs = keep.tile([P, 2, D], U8, name="qs", align_bytes=64)
+        nc.vector.tensor_copy(out=spread(qg[0][:]), in_=gather(q_raw[0][:]))
+        nc.scalar.copy(spread(qg[1][:, 0:256, :]), gather(q_raw[1][:, :, 0:256]))
+        nc.vector.tensor_copy(out=spread(qg[1][:, 256:512, :]), in_=gather(q_raw[1][:, :, 256:512]))
+        for g in range(2):
+            nc.vector.quantize_mx(
+                out=qc[:, g, :].bitcast(X4), scales=qs[:, g, :], in_=qg[g][:].rearrange("p c t -> p (c t)")
+            )
+
+        dsc = [keep.tile([P, 2, UNIT], U32, name="dsc%d" % k, align_bytes=64) for k in range(M // UNIT)]
+        dss = [keep.tile([P, 2, UNIT], U8, name="dss%d" % k, align_bytes=64) for k in range(M // UNIT)]
+        grouped = {}
+
+        def ds_interleave(k):
+            c = [i for i, (a, w) in enumerate(CHUNKS) if a <= k * UNIT < a + w][0]
+            off = k * UNIT - CHUNKS[c][0]
+            g0 = work.tile([P, UNIT, 4], BF16, name="g0", align_bytes=64)
+            g1 = work.tile([P, UNIT, 4], BF16, name="g1", align_bytes=64)
+            nc.vector.tensor_copy(out=spread(g0[:]), in_=gather(ds_raw[c][:, 0, :, off : off + UNIT]))
+            nc.scalar.copy(spread(g1[:]), gather(ds_raw[c][:, 1, :, off : off + UNIT]))
+            grouped[k] = (g0, g1)
+
+        def ds_quantize(k):
+            for g in range(2):
+                nc.vector.quantize_mx(
+                    out=dsc[k][:, g, :].bitcast(X4),
+                    scales=dss[k][:, g, :],
+                    in_=grouped[k][g][:].rearrange("p c t -> p (c t)"),
+                )
+
+        ssq = [keep.tile([P, 2], F32, name="ssq%d" % c) for c in range(TILES // 2)]
+        zz = [keep.tile([P, 2], F32, name="zz%d" % c) for c in range(TILES // 2)]
+        ir = [keep.tile([P, 2], F32, name="ir%d" % c) for c in range(TILES // 2)]
+        k2 = [keep.tile([P, 2], F32, name="k2%d" % c) for c in range(TILES // 2)]
+
+        def u_square(i):
+            c, h = divmod(i, 2)
+            sq = work.tile([P, D], BF16, name="sq")
+            nc.scalar.activation(sq[:], u_raw[c][:, h, :], ACT.Square, accum_out=ssq[c][:, h : h + 1])
+
+        def u_stats(c):
+            nc.gpsimd.tensor_scalar(zz[c][:], ssq[c][:], D * EPS, 1.0, ALU.add, ALU.mult)
+            nc.gpsimd.tensor_tensor(ir[c][:], zz[c][:], expo[:], ALU.pow)
+            nc.gpsimd.tensor_tensor(zz[c][:], ir[c][:], ir[c][:], ALU.mult)
+            nc.gpsimd.tensor_scalar(k2[c][:], zz[c][:], -1.0, 0.0, ALU.mult, ALU.add)
+
+        dk, gr, cu, tr, dzg, dzc, dzs = {}, {}, {}, {}, {}, {}, {}
+        gam = keep.tile([P, D], F32, name="gam")
+        wkc = keep.tile([P, E], U32, name="wkc", align_bytes=64)
+        wks = keep.tile([P, E], U8, name="wks", align_bytes=64)
+        pls = keep.tile([P, 2, M], U8, name="pls", align_bytes=64)
+
+        def mx1(i):
+            k, h = divmod(i, 2)
+            bank = ps_dk.tile([P, D], F32, name="dk")
+            for g in range(2):
+                nc.tensor.matmul_mx(
+                    out=bank[:],
+                    lhsT=dsc[k][:, g, h * P : (h + 1) * P].bitcast(X4),
+                    lhsT_scale=dss[k][:, g, h * P : (h + 1) * P],
+                    rhs=qc[:, g, :].bitcast(X4),
+                    rhs_scale=qs[:, g, :],
+                    start=(g == 0),
+                    stop=(g == 1),
+                )
+            dk[i] = bank
+
+        def p2(i):
+            c, h = divmod(i, 2)
+            t = work.tile([P, D], F32, name="gr")
+            nc.vector.scalar_tensor_tensor(t[:], dk[i][:], ir[c][:, h : h + 1], gam[:], ALU.mult, ALU.mult)
+            gr[i] = t
+
+        def p1(i):
+            c, h = divmod(i, 2)
+            junk = work.tile([P, D], BF16, name="junk")
+            ncoef = work.tile([P, 1], F32, name="ncoef")
+            nc.vector.scalar_tensor_tensor(
+                junk[:], gr[i][:], k2[c][:, h : h + 1], u_raw[c][:, h, :], ALU.mult, ALU.mult, accum_out=ncoef[:]
+            )
+            t = work.tile([P, 4, P], F32, name="cu")
+            nc.gpsimd.tensor_scalar(
+                t[:], u_raw[c][:, h, :].rearrange("m (p t) -> m t p", t=4), ncoef[:], 1.0, ALU.mult, ALU.mult
+            )
+            cu[i] = t
+
+        def transposes(i):
+            bank = ps_tr.tile([P, 4, P], F32, name="tr")
+            for t in range(4):
+                nc.tensor.matmul(bank[:, t, :], gr[i][:, t:D:4], ident[:], start=True, stop=False, is_transpose=True)
+                nc.tensor.matmul(bank[:, t, :], cu[i][:, t, :], ident[:], start=False, stop=True, is_transpose=True)
+            tr[i] = bank
+
+        def times_l(i):
+            t = work.tile([P, P, 4], BF16, name="dzg", align_bytes=64)
+            nc.vector.tensor_tensor(
+                t[:],
+                tr[i][:].rearrange("p t m -> p m t"),
+                l_col[:].unsqueeze(1).to_broadcast([P, P, 4]),
+                ALU.mult,
+            )
+            dzg[i] = t
+
+        def quantize_dz(i):
+            c = work.tile([P, P], U32, name="dzc", align_bytes=64)
+            s = work.tile([P, P], U8, name="dzs", align_bytes=64)
+            nc.vector.quantize_mx(out=c[:].bitcast(X4), scales=s[:], in_=dzg[i][:].rearrange("p m t -> p (m t)"))
+            dzc[i], dzs[i] = c, s
+
+        o_sb, p_sb, p_codes = {}, {}, {}
+
+        def mx2(i):
+            banks = []
+            for g in range(2):
+                pl = ps_out.tile([P, 4, P], F32, name="ob")
+                for t in range(4):
+                    cols = slice(g * 512 + t * P, g * 512 + (t + 1) * P)
+                    nc.tensor.matmul_mx(
+                        out=pl[:, t, :],
+                        lhsT=wkc[:, cols].bitcast(X4),
+                        lhsT_scale=wks[:, cols],
+                        rhs=dzc[i][:].bitcast(X4),
+                        rhs_scale=dzs[i][:],
+                        start=True,
+                        stop=True,
+                    )
+                ob = ps_out.tile([P, 4, P], F32, name="ob")
+                cols = slice(g * 512, (g + 1) * 512)
+                nc.tensor.matmul_mx(
+                    out=ob[:].rearrange("p t m -> p (t m)"),
+                    lhsT=dzc[i][:].bitcast(X4),
+                    lhsT_scale=dzs[i][:],
+                    rhs=wkc[:, cols].bitcast(X4),
+                    rhs_scale=wks[:, cols],
+                    start=True,
+                    stop=True,
+                )
+                banks.append((pl, ob))
+            o = work.tile([P, 2, P, 4], F32, name="o")
+            p = work.tile([P, 2, P, 4], BF16, name="p", align_bytes=64)
+            for g in range(2):
+                pl, ob = banks[g]
+                if i >= TILES - 2:
+                    nc.vector.tensor_copy(out=p[:, g, :, :], in_=pl[:].rearrange("p t m -> p m t"))
+                else:
+                    nc.scalar.copy(p[:, g, :, :], pl[:].rearrange("p t m -> p m t"))
+                nc.scalar.copy(o[:, g, :, :], ob[:].rearrange("m t p -> m p t"))
+            nc.sync.dma_start(out=out_0[i * P : (i + 1) * P, :], in_=o[:].rearrange("m g p t -> m (g p t)"))
+            p_sb[i] = p
+
+        def quantize_planes(i):
+            c, h = divmod(i, 2)
+            if h == 0:
+                p_codes[c] = work.tile([P, 2, 2 * P], U32, name="pc", align_bytes=64)
+            for g in range(2):
+                nc.vector.quantize_mx(
+                    out=p_codes[c][:, g, h * P : (h + 1) * P].bitcast(X4),
+                    scales=pls[:, g, i * P : (i + 1) * P],
+                    in_=p_sb[i][:, g, :, :].rearrange("p m t -> p (m t)"),
+                )
+            if h == 1:
+                nc.sync.dma_start(
+                    out=out_1[:, :, 256 * c : 256 * (c + 1), :].rearrange("g p m t -> p g (m t)").bitcast(I32),
+                    in_=p_codes[c][:].bitcast(I32),
+                )
+            if i % 8 == 7:
+                cols = slice((i - 7) * P, (i + 1) * P)
+                for quad in range(4):
+                    nc.sync.dma_start(
+                        out=out_2[:, 4 * quad : 4 * quad + 4, cols].rearrange("g r m -> r g m").bitcast(I32),
+                        in_=pls[32 * quad : 32 * quad + 4, :, cols].bitcast(I32),
+                    )
+
+        ds_interleave(0)
+        ds_quantize(0)
+        mx1(0)
+        gbank = ps_tr.tile([P, 4, P], F32, name="tr")
+        nc.tensor.matmul(gbank[:].rearrange("p t m -> p (t m)"), ones[:], g_row[:], start=True, stop=True)
+        nc.scalar.copy(gam[:], gbank[:].rearrange("p t m -> p (t m)"))
+        for i in range(2):
+            u_square(i)
+        u_stats(0)
+        words = wk_raw[:].rearrange("p g t d -> p (g t d)").bitcast(F32)
+        wg = keep.tile([P, E, 4], BF16, name="wg", align_bytes=64)
+        wbanks = []
+        for b in range(4):
+            bank = ps_out.tile([P, 4, P], F32, name="ob")
+            for s in range(4):
+                base = (2 * b + s // 2) * 256
+                nc.tensor.transpose(bank[:, s, :], words[:, base + s % 2 : base + 256 : 2], ident[:])
+            wbanks.append(bank)
+        ds_interleave(1)
+        for b in range(4):
+            dst = (
+                wg[:, 256 * b : 256 * (b + 1), :]
+                .rearrange("p c k -> p (c k)")
+                .bitcast(F32)
+                .rearrange("p (a c w) -> p a c w", a=2, w=2)
+            )
+            srcv = wbanks[b][:].rearrange("p (a w) c -> p a c w", a=2)
+            if b % 2 == 0:
+                nc.vector.tensor_copy(out=dst, in_=srcv)
+            else:
+                nc.scalar.copy(dst, srcv)
+        ds_quantize(1)
+        for g in range(2):
+            cols = slice(512 * g, 512 * (g + 1))
+            nc.vector.quantize_mx(
+                out=wkc[:, cols].bitcast(X4), scales=wks[:, cols], in_=wg[:, cols, :].rearrange("p c k -> p (c k)")
+            )
+        for i in range(2, 4):
+            u_square(i)
+        u_stats(1)
+
+        for s in range(TILES + 3):
+            if s < TILES:
+                p2(s)
+            if 1 <= s <= TILES:
+                transposes(s - 1)
+            if s >= 3:
+                quantize_planes(s - 3)
+            if s < TILES:
+                p1(s)
+            if s + 1 < TILES:
+                mx1(s + 1)
+            if 1 <= s <= TILES:
+                times_l(s - 1)
+            if 2 <= s <= TILES + 1:
+                mx2(s - 2)
+            unit = s // 2 + 2
+            if unit < M // UNIT:
+                if s % 2 == 0:
+                    ds_interleave(unit)
+                else:
+                    ds_quantize(unit)
+            if 1 <= s <= TILES:
+                quantize_dz(s - 1)
+            if s + 4 < TILES:
+                u_square(s + 4)
+                if s % 2 == 1:
+                    u_stats((s + 4) // 2)

@@ -17,6 +17,16 @@ ACT = mybir.ActivationFunctionType
 
 P = 128
 EPS = 1e-6
+Q_DVE = 320
+CUB = 4
+ILV = {0: 'v', 1: 'a', (6, 1): 'v', (3, 1): 'v', (5, 1): 'a', (7, 1): 'a', (4, 1): 'a', (0, 1): 'v', (6, 0): 'v', (2, 1): 'a', (3, 0): 'v', (0, 0): 'v', (2, 0): 'v', (1, 0): 'v', (1, 1): 'a', (4, 0): 'v', (5, 0): 'v'}
+DVE_PLANES = [3, 7, 13, 14, 15]
+DSL = 3
+WK0 = 0
+DSI = {0: [1], 1: [], 3: [], 5: [], 7: [5], 9: [6], 11: [7], 4: [3], 2: [2], 10: [], 8: [], 6: [4]}
+SQ = {0: [3, 2], 1: [4, 5], 2: [6, 7, 8], 3: [10, 9], 4: [], 5: [11], 6: [12], 7: [], 8: [], 9: [13], 10: [15, 14]}
+ST = {6: 3, 10: 4, 1: 1, 2: 2}
+GROUPS = [(0, 2), (2, 2), (4, 4), (8, 4), (12, 4)]
 TILES = M // P
 UNIT = 256
 CHUNKS = [(0, 256), (256, 256), (512, 512), (1024, 512), (1536, 512)]
@@ -40,7 +50,8 @@ def tile_ia3scaledqknormkeybackwardtoinput_x1_kernel(tc, ds, q, u, gamma, l, wk,
         ones = keep.tile([P, P], BF16, name="ones")
         l_col = keep.tile([P, 4], BF16, name="l_col")
         ident = keep.tile([P, P], F32, name="ident")
-        expo = keep.tile([P, 2], F32, name="expo")
+        warm = keep.tile([P, 1], F32, name="warm")
+        eps = keep.tile([P, 1], F32, name="eps")
 
         def load_ds(c):
             a, w = CHUNKS[c]
@@ -55,17 +66,22 @@ def tile_ia3scaledqknormkeybackwardtoinput_x1_kernel(tc, ds, q, u, gamma, l, wk,
                 out=u_raw[c][:], in_=u[256 * c : 256 * (c + 1), :].rearrange("(i p) d -> p i d", i=2)
             )
 
-        nc.gpsimd.memset(g_row[:], 0.0)
-        nc.gpsimd.memset(ones[:], 1.0)
-        nc.gpsimd.memset(expo[:], -0.5)
+        nc.vector.memset(g_row[:], 0.0)
+        nc.vector.memset(ones[:], 1.0)
+        nc.vector.memset(warm[:], 1.0)
+        nc.vector.tensor_scalar(eps[:], warm[:], 0.0, D * EPS, ALU.mult, ALU.add)
+        nc.scalar.activation(warm[:], warm[:], ACT.Sqrt)
         make_identity(nc, ident[:])
         nc.scalar.dma_start(out=l_col[:], in_=l.rearrange("(p t) -> p t", t=4))
         nc.scalar.dma_start(out=g_row[0:1, :], in_=gamma.rearrange("(o d) -> o d", o=1))
 
-        for g in range(2):
+        def load_q(g):
             nc.sync.dma_start(
                 out=q_raw[g][:], in_=q[512 * g : 512 * (g + 1), :].rearrange("(p j) d -> p j d", j=4)
             )
+
+        load_q(0)
+        load_q(1)
         load_ds(0)
         load_u(0)
         nc.sync.dma_start(out=wk_raw[:], in_=wk.rearrange("(g p t) d -> p g t d", g=2, t=4))
@@ -87,12 +103,31 @@ def tile_ia3scaledqknormkeybackwardtoinput_x1_kernel(tc, ds, q, u, gamma, l, wk,
         def gather(x):
             return x.rearrange("p t (c i) -> p c t i", i=4)
 
+        ssq = [keep.tile([P, w], F32, name="ssq%d" % c) for c, (a, w) in enumerate(GROUPS)]
+        zz = [keep.tile([P, w], F32, name="zz%d" % c) for c, (a, w) in enumerate(GROUPS)]
+        ir = [keep.tile([P, w], F32, name="ir%d" % c) for c, (a, w) in enumerate(GROUPS)]
+        k2 = [keep.tile([P, w], F32, name="k2%d" % c) for c, (a, w) in enumerate(GROUPS)]
+
+        def column(x, i):
+            c = [n for n, (a, w) in enumerate(GROUPS) if a <= i < a + w][0]
+            return x[c][:, i - GROUPS[c][0] : i - GROUPS[c][0] + 1]
+
+        def u_square(i):
+            c, h = divmod(i, 2)
+            sq = work.tile([P, D], BF16, name="sq")
+            nc.scalar.activation(sq[:], u_raw[c][:, h, :], ACT.Square, accum_out=column(ssq, i))
+
+        def u_stats(c):
+            nc.scalar.activation(zz[c][:], ssq[c][:], ACT.Sqrt, bias=eps[:])
+            nc.vector.reciprocal(ir[c][:], zz[c][:])
+            nc.vector.scalar_tensor_tensor(k2[c][:], ir[c][:], -1.0, ir[c][:], ALU.mult, ALU.mult)
+
         qg = [keep.tile([P, D, 4], BF16, name="qg%d" % g, align_bytes=64) for g in range(2)]
         qc = keep.tile([P, 2, D], U32, name="qc", align_bytes=64)
         qs = keep.tile([P, 2, D], U8, name="qs", align_bytes=64)
-        nc.vector.tensor_copy(out=spread(qg[0][:]), in_=gather(q_raw[0][:]))
-        nc.scalar.copy(spread(qg[1][:, 0:256, :]), gather(q_raw[1][:, :, 0:256]))
-        nc.vector.tensor_copy(out=spread(qg[1][:, 256:512, :]), in_=gather(q_raw[1][:, :, 256:512]))
+        for g in range(2):
+            nc.vector.tensor_copy(out=spread(qg[g][:, 0:Q_DVE, :]), in_=gather(q_raw[g][:, :, 0:Q_DVE]))
+            nc.scalar.copy(spread(qg[g][:, Q_DVE:D, :]), gather(q_raw[g][:, :, Q_DVE:D]))
         for g in range(2):
             nc.vector.quantize_mx(
                 out=qc[:, g, :].bitcast(X4), scales=qs[:, g, :], in_=qg[g][:].rearrange("p c t -> p (c t)")
@@ -105,10 +140,17 @@ def tile_ia3scaledqknormkeybackwardtoinput_x1_kernel(tc, ds, q, u, gamma, l, wk,
         def ds_interleave(k):
             c = [i for i, (a, w) in enumerate(CHUNKS) if a <= k * UNIT < a + w][0]
             off = k * UNIT - CHUNKS[c][0]
-            g0 = work.tile([P, UNIT, 4], BF16, name="g0", align_bytes=64)
-            g1 = work.tile([P, UNIT, 4], BF16, name="g1", align_bytes=64)
-            nc.vector.tensor_copy(out=spread(g0[:]), in_=gather(ds_raw[c][:, 0, :, off : off + UNIT]))
-            nc.scalar.copy(spread(g1[:]), gather(ds_raw[c][:, 1, :, off : off + UNIT]))
+            g0 = work.tile([P, UNIT, 4], BF16, bufs=4, name="g0", align_bytes=64)
+            g1 = work.tile([P, UNIT, 4], BF16, bufs=4, name="g1", align_bytes=64)
+            for g, t in ((0, g0), (1, g1)):
+                src = gather(ds_raw[c][:, g, :, off : off + UNIT])
+                eng = ILV.get((k, g), ILV[g])
+                if eng == "v":
+                    nc.vector.tensor_copy(out=spread(t[:]), in_=src)
+                elif eng == "a":
+                    nc.scalar.copy(spread(t[:]), src)
+                else:
+                    nc.gpsimd.tensor_scalar(spread(t[:]), src, 1.0, 1.0, ALU.mult, ALU.mult)
             grouped[k] = (g0, g1)
 
         def ds_quantize(k):
@@ -119,23 +161,7 @@ def tile_ia3scaledqknormkeybackwardtoinput_x1_kernel(tc, ds, q, u, gamma, l, wk,
                     in_=grouped[k][g][:].rearrange("p c t -> p (c t)"),
                 )
 
-        ssq = [keep.tile([P, 2], F32, name="ssq%d" % c) for c in range(TILES // 2)]
-        zz = [keep.tile([P, 2], F32, name="zz%d" % c) for c in range(TILES // 2)]
-        ir = [keep.tile([P, 2], F32, name="ir%d" % c) for c in range(TILES // 2)]
-        k2 = [keep.tile([P, 2], F32, name="k2%d" % c) for c in range(TILES // 2)]
-
-        def u_square(i):
-            c, h = divmod(i, 2)
-            sq = work.tile([P, D], BF16, name="sq")
-            nc.scalar.activation(sq[:], u_raw[c][:, h, :], ACT.Square, accum_out=ssq[c][:, h : h + 1])
-
-        def u_stats(c):
-            nc.gpsimd.tensor_scalar(zz[c][:], ssq[c][:], D * EPS, 1.0, ALU.add, ALU.mult)
-            nc.gpsimd.tensor_tensor(ir[c][:], zz[c][:], expo[:], ALU.pow)
-            nc.gpsimd.tensor_tensor(zz[c][:], ir[c][:], ir[c][:], ALU.mult)
-            nc.gpsimd.tensor_scalar(k2[c][:], zz[c][:], -1.0, 0.0, ALU.mult, ALU.add)
-
-        dk, gr, cu, tr, dzg, dzc, dzs = {}, {}, {}, {}, {}, {}, {}
+        dk, gr, cu, coef, tr, dzg, dzc, dzs = {}, {}, {}, {}, {}, {}, {}, {}
         gam = keep.tile([P, D], F32, name="gam")
         wkc = keep.tile([P, E], U32, name="wkc", align_bytes=64)
         wks = keep.tile([P, E], U8, name="wks", align_bytes=64)
@@ -157,22 +183,24 @@ def tile_ia3scaledqknormkeybackwardtoinput_x1_kernel(tc, ds, q, u, gamma, l, wk,
             dk[i] = bank
 
         def p2(i):
-            c, h = divmod(i, 2)
-            t = work.tile([P, D], F32, name="gr")
-            nc.vector.scalar_tensor_tensor(t[:], dk[i][:], ir[c][:, h : h + 1], gam[:], ALU.mult, ALU.mult)
+            t = work.tile([P, D], F32, bufs=6, name="gr")
+            nc.vector.scalar_tensor_tensor(t[:], dk[i][:], column(ir, i), gam[:], ALU.mult, ALU.mult)
             gr[i] = t
 
         def p1(i):
             c, h = divmod(i, 2)
-            junk = work.tile([P, D], BF16, name="junk")
-            ncoef = work.tile([P, 1], F32, name="ncoef")
+            junk = work.tile([P, D], BF16, bufs=3, name="junk")
+            ncoef = work.tile([P, 1], F32, bufs=6, name="ncoef")
             nc.vector.scalar_tensor_tensor(
-                junk[:], gr[i][:], k2[c][:, h : h + 1], u_raw[c][:, h, :], ALU.mult, ALU.mult, accum_out=ncoef[:]
+                junk[:], gr[i][:], column(k2, i), u_raw[c][:, h, :], ALU.mult, ALU.mult, accum_out=ncoef[:]
             )
-            t = work.tile([P, 4, P], F32, name="cu")
-            nc.gpsimd.tensor_scalar(
-                t[:], u_raw[c][:, h, :].rearrange("m (p t) -> m t p", t=4), ncoef[:], 1.0, ALU.mult, ALU.mult
-            )
+            coef[i] = ncoef
+
+        def cu_make(i):
+            c, h = divmod(i, 2)
+            t = work.tile([P, 4, P], F32, bufs=CUB, name="cu")
+            src = u_raw[c][:, h, :].rearrange("m (p t) -> m t p", t=4)
+            nc.scalar.activation(t[:], src, ACT.Copy, scale=coef[i][:])
             cu[i] = t
 
         def transposes(i):
@@ -183,7 +211,7 @@ def tile_ia3scaledqknormkeybackwardtoinput_x1_kernel(tc, ds, q, u, gamma, l, wk,
             tr[i] = bank
 
         def times_l(i):
-            t = work.tile([P, P, 4], BF16, name="dzg", align_bytes=64)
+            t = work.tile([P, P, 4], BF16, bufs=5, name="dzg", align_bytes=64)
             nc.vector.tensor_tensor(
                 t[:],
                 tr[i][:].rearrange("p t m -> p m t"),
@@ -193,12 +221,12 @@ def tile_ia3scaledqknormkeybackwardtoinput_x1_kernel(tc, ds, q, u, gamma, l, wk,
             dzg[i] = t
 
         def quantize_dz(i):
-            c = work.tile([P, P], U32, name="dzc", align_bytes=64)
-            s = work.tile([P, P], U8, name="dzs", align_bytes=64)
+            c = work.tile([P, P], U32, bufs=6, name="dzc", align_bytes=64)
+            s = work.tile([P, P], U8, bufs=6, name="dzs", align_bytes=64)
             nc.vector.quantize_mx(out=c[:].bitcast(X4), scales=s[:], in_=dzg[i][:].rearrange("p m t -> p (m t)"))
             dzc[i], dzs[i] = c, s
 
-        o_sb, p_sb, p_codes = {}, {}, {}
+        ob_banks, p_sb, p_codes = {}, {}, {}
 
         def mx2(i):
             banks = []
@@ -227,11 +255,15 @@ def tile_ia3scaledqknormkeybackwardtoinput_x1_kernel(tc, ds, q, u, gamma, l, wk,
                     stop=True,
                 )
                 banks.append((pl, ob))
+            ob_banks[i] = banks
+
+        def evacuate(i):
+            banks = ob_banks[i]
             o = work.tile([P, 2, P, 4], F32, name="o")
-            p = work.tile([P, 2, P, 4], BF16, name="p", align_bytes=64)
+            p = work.tile([P, 2, P, 4], BF16, bufs=5, name="p", align_bytes=64)
             for g in range(2):
                 pl, ob = banks[g]
-                if i >= TILES - 2:
+                if i in DVE_PLANES:
                     nc.vector.tensor_copy(out=p[:, g, :, :], in_=pl[:].rearrange("p t m -> p m t"))
                 else:
                     nc.scalar.copy(p[:, g, :, :], pl[:].rearrange("p t m -> p m t"))
@@ -262,71 +294,74 @@ def tile_ia3scaledqknormkeybackwardtoinput_x1_kernel(tc, ds, q, u, gamma, l, wk,
                         in_=pls[32 * quad : 32 * quad + 4, :, cols].bitcast(I32),
                     )
 
-        ds_interleave(0)
-        ds_quantize(0)
-        mx1(0)
-        gbank = ps_tr.tile([P, 4, P], F32, name="tr")
-        nc.tensor.matmul(gbank[:].rearrange("p t m -> p (t m)"), ones[:], g_row[:], start=True, stop=True)
-        nc.scalar.copy(gam[:], gbank[:].rearrange("p t m -> p (t m)"))
-        for i in range(2):
-            u_square(i)
-        u_stats(0)
         words = wk_raw[:].rearrange("p g t d -> p (g t d)").bitcast(F32)
         wg = keep.tile([P, E, 4], BF16, name="wg", align_bytes=64)
         wbanks = []
-        for b in range(4):
-            bank = ps_out.tile([P, 4, P], F32, name="ob")
-            for s in range(4):
-                base = (2 * b + s // 2) * 256
-                nc.tensor.transpose(bank[:, s, :], words[:, base + s % 2 : base + 256 : 2], ident[:])
-            wbanks.append(bank)
-        ds_interleave(1)
-        for b in range(4):
+
+        def wk_transposes():
+            for b in range(4):
+                bank = ps_out.tile([P, 4, P], F32, name="ob")
+                for s in range(4):
+                    base = (2 * b + s // 2) * 256
+                    nc.tensor.transpose(bank[:, s, :], words[:, base + s % 2 : base + 256 : 2], ident[:])
+                wbanks.append(bank)
+
+        def wk_copy(b, copy):
             dst = (
                 wg[:, 256 * b : 256 * (b + 1), :]
                 .rearrange("p c k -> p (c k)")
                 .bitcast(F32)
                 .rearrange("p (a c w) -> p a c w", a=2, w=2)
             )
-            srcv = wbanks[b][:].rearrange("p (a w) c -> p a c w", a=2)
-            if b % 2 == 0:
-                nc.vector.tensor_copy(out=dst, in_=srcv)
-            else:
-                nc.scalar.copy(dst, srcv)
-        ds_quantize(1)
-        for g in range(2):
+            copy(dst, wbanks[b][:].rearrange("p (a w) c -> p a c w", a=2))
+
+        def wk_quantize(g):
             cols = slice(512 * g, 512 * (g + 1))
             nc.vector.quantize_mx(
                 out=wkc[:, cols].bitcast(X4), scales=wks[:, cols], in_=wg[:, cols, :].rearrange("p c k -> p (c k)")
             )
-        for i in range(2, 4):
-            u_square(i)
-        u_stats(1)
 
-        for s in range(TILES + 3):
-            if s < TILES:
-                p2(s)
-            if 1 <= s <= TILES:
-                transposes(s - 1)
-            if s >= 3:
-                quantize_planes(s - 3)
-            if s < TILES:
-                p1(s)
-            if s + 1 < TILES:
-                mx1(s + 1)
-            if 1 <= s <= TILES:
-                times_l(s - 1)
-            if 2 <= s <= TILES + 1:
-                mx2(s - 2)
-            unit = s // 2 + 2
-            if unit < M // UNIT:
-                if s % 2 == 0:
-                    ds_interleave(unit)
-                else:
-                    ds_quantize(unit)
-            if 1 <= s <= TILES:
-                quantize_dz(s - 1)
-            if s + 4 < TILES:
-                u_square(s + 4)
-                if s % 2 == 1:
-                    u_stats((s + 4) // 2)
+        ds_interleave(0)
+        gbank = ps_tr.tile([P, 4, P], F32, name="tr")
+        nc.tensor.matmul(gbank[:].rearrange("p t m -> p (t m)"), ones[:], g_row[:], start=True, stop=True)
+        nc.scalar.copy(gam[:], gbank[:].rearrange("p t m -> p (t m)"))
+        u_square(0)
+        u_square(1)
+        ds_quantize(0)
+        u_stats(0)
+        mx1(0)
+        mx1(1)
+        wk_transposes()
+
+
+        LAG = {'p2': 0, 'tr': 1, 'mx1': -1, 'evl': 1, 'p1': 0, 'cu': 0, 'mx2': 2, 'ev': 2, 'qpl': 3, 'qdz': 1}
+        ORDER = ['p2', 'ds', 'tr', 'mx1', 'wk', 'p1', 'evl', 'qpl', 'sq', 'mx2', 'qdz', 'cu', 'dsq', 'ev']
+        FN = dict(p2=p2, tr=transposes, mx1=mx1, evl=times_l, p1=p1, cu=cu_make, mx2=mx2, ev=evacuate, qpl=quantize_planes, qdz=quantize_dz)
+        for s in range(0, TILES + LAG["qpl"]):
+            for name in ORDER:
+                if name in LAG:
+                    i = s - LAG[name]
+                    if 0 <= i < TILES and not (name == "mx1" and i < 2):
+                        FN[name](i)
+                elif name == "wk":
+                    if s == WK0:
+                        wk_copy(0, nc.vector.tensor_copy)
+                        wk_copy(1, nc.scalar.copy)
+                    if s == WK0 + 1:
+                        wk_copy(2, nc.vector.tensor_copy)
+                        wk_copy(3, nc.scalar.copy)
+                        wk_quantize(0)
+                    if s == WK0 + 2:
+                        wk_quantize(1)
+                elif name == "ds":
+                    for unit in DSI.get(s, []):
+                        ds_interleave(unit)
+                elif name == "dsq":
+                    unit = (s + DSL) // 2
+                    if 1 <= unit < M // UNIT and (s + DSL) % 2 == 1:
+                        ds_quantize(unit)
+                elif name == "sq":
+                    for i in SQ.get(s, []):
+                        u_square(i)
+                    if s in ST:
+                        u_stats(ST[s])

from contextlib import ExitStack

import concourse.mybir as mybir
from concourse.masks import make_identity

N, M, D, E = 1024, 2048, 512, 1024
FLOPS = 2 * N * M * D + 2 * M * D * E

F32 = mybir.dt.float32
BF16 = mybir.dt.bfloat16
U32 = mybir.dt.uint32
I32 = mybir.dt.int32
U8 = mybir.dt.uint8
X4 = mybir.dt.float8_e4m3fn_x4
ALU = mybir.AluOpType
ACT = mybir.ActivationFunctionType

P = 128
EPS = 1e-6
Q_DVE = 320
CUB = 4
ILV = {0: 'v', 1: 'a', (6, 1): 'v', (3, 1): 'v', (5, 1): 'a', (7, 1): 'a', (4, 1): 'a', (0, 1): 'v', (6, 0): 'v', (2, 1): 'a', (3, 0): 'v', (0, 0): 'v', (2, 0): 'v', (1, 0): 'v', (1, 1): 'a', (4, 0): 'v', (5, 0): 'v'}
DVE_PLANES = [3, 7, 13, 14, 15]
DSL = 3
WK0 = 0
DSI = {0: [1], 1: [], 3: [], 5: [], 7: [5], 9: [6], 11: [7], 4: [3], 2: [2], 10: [], 8: [], 6: [4]}
SQ = {0: [3, 2], 1: [4, 5], 2: [6, 7, 8], 3: [10, 9], 4: [], 5: [11], 6: [12], 7: [], 8: [], 9: [13], 10: [15, 14]}
ST = {6: 3, 10: 4, 1: 1, 2: 2}
GROUPS = [(0, 2), (2, 2), (4, 4), (8, 4), (12, 4)]
TILES = M // P
UNIT = 256
CHUNKS = [(0, 256), (256, 256), (512, 512), (1024, 512), (1536, 512)]


def tile_ia3scaledqknormkeybackwardtoinput_x1_kernel(tc, ds, q, u, gamma, l, wk, out_0, out_1, out_2):
    nc = tc.nc
    with ExitStack() as ctx:
        keep = ctx.enter_context(tc.tile_pool(name="keep", bufs=1))
        work = ctx.enter_context(tc.tile_pool(name="work", bufs=3))
        ps_dk = ctx.enter_context(tc.psum_pool(name="ps_dk", bufs=2))
        ps_tr = ctx.enter_context(tc.psum_pool(name="ps_tr", bufs=2))
        ps_out = ctx.enter_context(tc.psum_pool(name="ps_out", bufs=4))
        ctx.enter_context(tc.manual_schedule())

        q_raw = [keep.tile([P, 4, D], BF16, name="q_raw%d" % g) for g in range(2)]
        ds_raw = [keep.tile([P, 2, 4, w], BF16, name="ds_raw%d" % c) for c, (a, w) in enumerate(CHUNKS)]
        u_raw = [keep.tile([P, 2, D], BF16, name="u_raw%d" % c) for c in range(TILES // 2)]
        wk_raw = keep.tile([P, 2, 4, D], BF16, name="wk_raw")
        g_row = keep.tile([P, D], BF16, name="g_row")
        ones = keep.tile([P, P], BF16, name="ones")
        l_col = keep.tile([P, 4], BF16, name="l_col")
        ident = keep.tile([P, P], F32, name="ident")
        warm = keep.tile([P, 1], F32, name="warm")
        eps = keep.tile([P, 1], F32, name="eps")

        def load_ds(c):
            a, w = CHUNKS[c]
            for g in range(2):
                nc.sync.dma_start(
                    out=ds_raw[c][:, g, :, :],
                    in_=ds[512 * g : 512 * (g + 1), a : a + w].rearrange("(p j) m -> p j m", j=4),
                )

        def load_u(c):
            nc.sync.dma_start(
                out=u_raw[c][:], in_=u[256 * c : 256 * (c + 1), :].rearrange("(i p) d -> p i d", i=2)
            )

        nc.vector.memset(g_row[:], 0.0)
        nc.vector.memset(ones[:], 1.0)
        nc.vector.memset(warm[:], 1.0)
        nc.vector.tensor_scalar(eps[:], warm[:], 0.0, D * EPS, ALU.mult, ALU.add)
        nc.scalar.activation(warm[:], warm[:], ACT.Sqrt)
        make_identity(nc, ident[:])
        nc.scalar.dma_start(out=l_col[:], in_=l.rearrange("(p t) -> p t", t=4))
        nc.scalar.dma_start(out=g_row[0:1, :], in_=gamma.rearrange("(o d) -> o d", o=1))

        def load_q(g):
            nc.sync.dma_start(
                out=q_raw[g][:], in_=q[512 * g : 512 * (g + 1), :].rearrange("(p j) d -> p j d", j=4)
            )

        load_q(0)
        load_q(1)
        load_ds(0)
        load_u(0)
        nc.sync.dma_start(out=wk_raw[:], in_=wk.rearrange("(g p t) d -> p g t d", g=2, t=4))
        load_ds(1)
        load_u(1)
        load_ds(2)
        load_u(2)
        load_u(3)
        load_ds(3)
        load_u(4)
        load_u(5)
        load_ds(4)
        load_u(6)
        load_u(7)

        def spread(x):
            return x.rearrange("p (c i) t -> p c t i", i=4)

        def gather(x):
            return x.rearrange("p t (c i) -> p c t i", i=4)

        ssq = [keep.tile([P, w], F32, name="ssq%d" % c) for c, (a, w) in enumerate(GROUPS)]
        zz = [keep.tile([P, w], F32, name="zz%d" % c) for c, (a, w) in enumerate(GROUPS)]
        ir = [keep.tile([P, w], F32, name="ir%d" % c) for c, (a, w) in enumerate(GROUPS)]
        k2 = [keep.tile([P, w], F32, name="k2%d" % c) for c, (a, w) in enumerate(GROUPS)]

        def column(x, i):
            c = [n for n, (a, w) in enumerate(GROUPS) if a <= i < a + w][0]
            return x[c][:, i - GROUPS[c][0] : i - GROUPS[c][0] + 1]

        def u_square(i):
            c, h = divmod(i, 2)
            sq = work.tile([P, D], BF16, name="sq")
            nc.scalar.activation(sq[:], u_raw[c][:, h, :], ACT.Square, accum_out=column(ssq, i))

        def u_stats(c):
            nc.scalar.activation(zz[c][:], ssq[c][:], ACT.Sqrt, bias=eps[:])
            nc.vector.reciprocal(ir[c][:], zz[c][:])
            nc.vector.scalar_tensor_tensor(k2[c][:], ir[c][:], -1.0, ir[c][:], ALU.mult, ALU.mult)

        qg = [keep.tile([P, D, 4], BF16, name="qg%d" % g, align_bytes=64) for g in range(2)]
        qc = keep.tile([P, 2, D], U32, name="qc", align_bytes=64)
        qs = keep.tile([P, 2, D], U8, name="qs", align_bytes=64)
        for g in range(2):
            nc.vector.tensor_copy(out=spread(qg[g][:, 0:Q_DVE, :]), in_=gather(q_raw[g][:, :, 0:Q_DVE]))
            nc.scalar.copy(spread(qg[g][:, Q_DVE:D, :]), gather(q_raw[g][:, :, Q_DVE:D]))
        for g in range(2):
            nc.vector.quantize_mx(
                out=qc[:, g, :].bitcast(X4), scales=qs[:, g, :], in_=qg[g][:].rearrange("p c t -> p (c t)")
            )

        dsc = [keep.tile([P, 2, UNIT], U32, name="dsc%d" % k, align_bytes=64) for k in range(M // UNIT)]
        dss = [keep.tile([P, 2, UNIT], U8, name="dss%d" % k, align_bytes=64) for k in range(M // UNIT)]
        grouped = {}

        def ds_interleave(k):
            c = [i for i, (a, w) in enumerate(CHUNKS) if a <= k * UNIT < a + w][0]
            off = k * UNIT - CHUNKS[c][0]
            g0 = work.tile([P, UNIT, 4], BF16, bufs=4, name="g0", align_bytes=64)
            g1 = work.tile([P, UNIT, 4], BF16, bufs=4, name="g1", align_bytes=64)
            for g, t in ((0, g0), (1, g1)):
                src = gather(ds_raw[c][:, g, :, off : off + UNIT])
                eng = ILV.get((k, g), ILV[g])
                if eng == "v":
                    nc.vector.tensor_copy(out=spread(t[:]), in_=src)
                elif eng == "a":
                    nc.scalar.copy(spread(t[:]), src)
                else:
                    nc.gpsimd.tensor_scalar(spread(t[:]), src, 1.0, 1.0, ALU.mult, ALU.mult)
            grouped[k] = (g0, g1)

        def ds_quantize(k):
            for g in range(2):
                nc.vector.quantize_mx(
                    out=dsc[k][:, g, :].bitcast(X4),
                    scales=dss[k][:, g, :],
                    in_=grouped[k][g][:].rearrange("p c t -> p (c t)"),
                )

        dk, gr, cu, coef, tr, dzg, dzc, dzs = {}, {}, {}, {}, {}, {}, {}, {}
        gam = keep.tile([P, D], F32, name="gam")
        wkc = keep.tile([P, E], U32, name="wkc", align_bytes=64)
        wks = keep.tile([P, E], U8, name="wks", align_bytes=64)
        pls = keep.tile([P, 2, M], U8, name="pls", align_bytes=64)

        def mx1(i):
            k, h = divmod(i, 2)
            bank = ps_dk.tile([P, D], F32, name="dk")
            for g in range(2):
                nc.tensor.matmul_mx(
                    out=bank[:],
                    lhsT=dsc[k][:, g, h * P : (h + 1) * P].bitcast(X4),
                    lhsT_scale=dss[k][:, g, h * P : (h + 1) * P],
                    rhs=qc[:, g, :].bitcast(X4),
                    rhs_scale=qs[:, g, :],
                    start=(g == 0),
                    stop=(g == 1),
                )
            dk[i] = bank

        def p2(i):
            t = work.tile([P, D], F32, bufs=6, name="gr")
            nc.vector.scalar_tensor_tensor(t[:], dk[i][:], column(ir, i), gam[:], ALU.mult, ALU.mult)
            gr[i] = t

        def p1(i):
            c, h = divmod(i, 2)
            junk = work.tile([P, D], BF16, bufs=3, name="junk")
            ncoef = work.tile([P, 1], F32, bufs=6, name="ncoef")
            nc.vector.scalar_tensor_tensor(
                junk[:], gr[i][:], column(k2, i), u_raw[c][:, h, :], ALU.mult, ALU.mult, accum_out=ncoef[:]
            )
            coef[i] = ncoef

        def cu_make(i):
            c, h = divmod(i, 2)
            t = work.tile([P, 4, P], F32, bufs=CUB, name="cu")
            src = u_raw[c][:, h, :].rearrange("m (p t) -> m t p", t=4)
            nc.scalar.activation(t[:], src, ACT.Copy, scale=coef[i][:])
            cu[i] = t

        def transposes(i):
            bank = ps_tr.tile([P, 4, P], F32, name="tr")
            for t in range(4):
                nc.tensor.matmul(bank[:, t, :], gr[i][:, t:D:4], ident[:], start=True, stop=False, is_transpose=True)
                nc.tensor.matmul(bank[:, t, :], cu[i][:, t, :], ident[:], start=False, stop=True, is_transpose=True)
            tr[i] = bank

        def times_l(i):
            t = work.tile([P, P, 4], BF16, bufs=5, name="dzg", align_bytes=64)
            nc.vector.tensor_tensor(
                t[:],
                tr[i][:].rearrange("p t m -> p m t"),
                l_col[:].unsqueeze(1).to_broadcast([P, P, 4]),
                ALU.mult,
            )
            dzg[i] = t

        def quantize_dz(i):
            c = work.tile([P, P], U32, bufs=6, name="dzc", align_bytes=64)
            s = work.tile([P, P], U8, bufs=6, name="dzs", align_bytes=64)
            nc.vector.quantize_mx(out=c[:].bitcast(X4), scales=s[:], in_=dzg[i][:].rearrange("p m t -> p (m t)"))
            dzc[i], dzs[i] = c, s

        ob_banks, p_sb, p_codes = {}, {}, {}

        def mx2(i):
            banks = []
            for g in range(2):
                pl = ps_out.tile([P, 4, P], F32, name="ob")
                for t in range(4):
                    cols = slice(g * 512 + t * P, g * 512 + (t + 1) * P)
                    nc.tensor.matmul_mx(
                        out=pl[:, t, :],
                        lhsT=wkc[:, cols].bitcast(X4),
                        lhsT_scale=wks[:, cols],
                        rhs=dzc[i][:].bitcast(X4),
                        rhs_scale=dzs[i][:],
                        start=True,
                        stop=True,
                    )
                ob = ps_out.tile([P, 4, P], F32, name="ob")
                cols = slice(g * 512, (g + 1) * 512)
                nc.tensor.matmul_mx(
                    out=ob[:].rearrange("p t m -> p (t m)"),
                    lhsT=dzc[i][:].bitcast(X4),
                    lhsT_scale=dzs[i][:],
                    rhs=wkc[:, cols].bitcast(X4),
                    rhs_scale=wks[:, cols],
                    start=True,
                    stop=True,
                )
                banks.append((pl, ob))
            ob_banks[i] = banks

        def evacuate(i):
            banks = ob_banks[i]
            o = work.tile([P, 2, P, 4], F32, name="o")
            p = work.tile([P, 2, P, 4], BF16, bufs=5, name="p", align_bytes=64)
            for g in range(2):
                pl, ob = banks[g]
                if i in DVE_PLANES:
                    nc.vector.tensor_copy(out=p[:, g, :, :], in_=pl[:].rearrange("p t m -> p m t"))
                else:
                    nc.scalar.copy(p[:, g, :, :], pl[:].rearrange("p t m -> p m t"))
                nc.scalar.copy(o[:, g, :, :], ob[:].rearrange("m t p -> m p t"))
            nc.sync.dma_start(out=out_0[i * P : (i + 1) * P, :], in_=o[:].rearrange("m g p t -> m (g p t)"))
            p_sb[i] = p

        def quantize_planes(i):
            c, h = divmod(i, 2)
            if h == 0:
                p_codes[c] = work.tile([P, 2, 2 * P], U32, name="pc", align_bytes=64)
            for g in range(2):
                nc.vector.quantize_mx(
                    out=p_codes[c][:, g, h * P : (h + 1) * P].bitcast(X4),
                    scales=pls[:, g, i * P : (i + 1) * P],
                    in_=p_sb[i][:, g, :, :].rearrange("p m t -> p (m t)"),
                )
            if h == 1:
                nc.sync.dma_start(
                    out=out_1[:, :, 256 * c : 256 * (c + 1), :].rearrange("g p m t -> p g (m t)").bitcast(I32),
                    in_=p_codes[c][:].bitcast(I32),
                )
            if i % 8 == 7:
                cols = slice((i - 7) * P, (i + 1) * P)
                for quad in range(4):
                    nc.sync.dma_start(
                        out=out_2[:, 4 * quad : 4 * quad + 4, cols].rearrange("g r m -> r g m").bitcast(I32),
                        in_=pls[32 * quad : 32 * quad + 4, :, cols].bitcast(I32),
                    )

        words = wk_raw[:].rearrange("p g t d -> p (g t d)").bitcast(F32)
        wg = keep.tile([P, E, 4], BF16, name="wg", align_bytes=64)
        wbanks = []

        def wk_transposes():
            for b in range(4):
                bank = ps_out.tile([P, 4, P], F32, name="ob")
                for s in range(4):
                    base = (2 * b + s // 2) * 256
                    nc.tensor.transpose(bank[:, s, :], words[:, base + s % 2 : base + 256 : 2], ident[:])
                wbanks.append(bank)

        def wk_copy(b, copy):
            dst = (
                wg[:, 256 * b : 256 * (b + 1), :]
                .rearrange("p c k -> p (c k)")
                .bitcast(F32)
                .rearrange("p (a c w) -> p a c w", a=2, w=2)
            )
            copy(dst, wbanks[b][:].rearrange("p (a w) c -> p a c w", a=2))

        def wk_quantize(g):
            cols = slice(512 * g, 512 * (g + 1))
            nc.vector.quantize_mx(
                out=wkc[:, cols].bitcast(X4), scales=wks[:, cols], in_=wg[:, cols, :].rearrange("p c k -> p (c k)")
            )

        ds_interleave(0)
        gbank = ps_tr.tile([P, 4, P], F32, name="tr")
        nc.tensor.matmul(gbank[:].rearrange("p t m -> p (t m)"), ones[:], g_row[:], start=True, stop=True)
        nc.scalar.copy(gam[:], gbank[:].rearrange("p t m -> p (t m)"))
        u_square(0)
        u_square(1)
        ds_quantize(0)
        u_stats(0)
        mx1(0)
        mx1(1)
        wk_transposes()


        LAG = {'p2': 0, 'tr': 1, 'mx1': -1, 'evl': 1, 'p1': 0, 'cu': 0, 'mx2': 2, 'ev': 2, 'qpl': 3, 'qdz': 1}
        ORDER = ['p2', 'ds', 'tr', 'mx1', 'wk', 'p1', 'evl', 'qpl', 'sq', 'mx2', 'qdz', 'cu', 'dsq', 'ev']
        FN = dict(p2=p2, tr=transposes, mx1=mx1, evl=times_l, p1=p1, cu=cu_make, mx2=mx2, ev=evacuate, qpl=quantize_planes, qdz=quantize_dz)
        for s in range(0, TILES + LAG["qpl"]):
            for name in ORDER:
                if name in LAG:
                    i = s - LAG[name]
                    if 0 <= i < TILES and not (name == "mx1" and i < 2):
                        FN[name](i)
                elif name == "wk":
                    if s == WK0:
                        wk_copy(0, nc.vector.tensor_copy)
                        wk_copy(1, nc.scalar.copy)
                    if s == WK0 + 1:
                        wk_copy(2, nc.vector.tensor_copy)
                        wk_copy(3, nc.scalar.copy)
                        wk_quantize(0)
                    if s == WK0 + 2:
                        wk_quantize(1)
                elif name == "ds":
                    for unit in DSI.get(s, []):
                        ds_interleave(unit)
                elif name == "dsq":
                    unit = (s + DSL) // 2
                    if 1 <= unit < M // UNIT and (s + DSL) % 2 == 1:
                        ds_quantize(unit)
                elif name == "sq":
                    for i in SQ.get(s, []):
                        u_square(i)
                    if s in ST:
                        u_stats(ST[s])
